import numpy as np
import ml_dtypes


def mxq(x, axis, fmt="e4m3"):
    dtype, down = {"e4m3": (ml_dtypes.float8_e4m3fn, 7), "e5m2": (ml_dtypes.float8_e5m2, 14)}[fmt]
    v = np.moveaxis(np.asarray(x, np.float32).astype(ml_dtypes.bfloat16).astype(np.float64), axis, -1)
    blocks = v.reshape(v.shape[:-1] + (-1, 32))
    amax = np.abs(blocks).max(-1, keepdims=True)
    byte = np.maximum(np.where(amax > 0, np.frexp(amax)[1] - 1 + 127, 0) - down, 1)
    scale = np.exp2(byte - 127.0)
    codes = (blocks / scale).astype(np.float32).astype(dtype).astype(np.float64)
    return np.moveaxis((codes * scale).reshape(v.shape), -1, axis)


WIDE = False


def mx_kscale(k):
    if not WIDE:
        return np.ones(k)
    levels = np.array([10, -10, 5, -5, 0])
    if k % 512:
        return np.exp2(np.random.permutation(np.resize(levels, k // 32))).repeat(32)
    a = np.empty((k // 512, 16))
    for p in range(k // 512):
        a[p, :8] = np.random.permutation(np.resize(levels, 8))
        for g in range(8):
            far = levels[np.abs(levels - a[p, g]) >= 10]
            a[p, g + 8] = far[np.random.randint(len(far))]
    return np.exp2(a.ravel()).repeat(32)


BF16 = ml_dtypes.bfloat16


def bf(x):
    return np.asarray(x, np.float32).astype(BF16)


def f64(x):
    return np.asarray(x).astype(np.float64)


E2M1 = np.array([0.0, 0.5, 1.0, 1.5, 2.0, 3.0, 4.0, 6.0, -0.0, -0.5, -1.0, -1.5, -2.0, -3.0, -4.0, -6.0])


def pack_weight(w, fmt):
    k, n = w.shape
    w = f64(bf(w)).reshape(k // 32, 32, n)
    amax = np.abs(w).max(1)
    if fmt == "e4m3":
        byte = np.frexp(amax)[1] - 1 + 127 - 7
    else:
        mant, ex = np.frexp(amax / 6.0)
        byte = np.where(mant > 0.5, ex, ex - 1) + 127
    byte = np.clip(np.where(amax > 0, byte, 1), 1, 254)
    scaled = (w * np.exp2(127.0 - byte)[:, None, :]).reshape(k, n).astype(np.float32)
    by_word = np.ascontiguousarray(scaled.reshape(k // 512, 128, 4, n).transpose(0, 1, 3, 2))
    if fmt == "e4m3":
        words = by_word.astype(ml_dtypes.float8_e4m3fn).view(np.uint8)
    else:
        c = by_word.astype(ml_dtypes.float4_e2m1fn).view(np.uint8) & 0xF
        words = c[..., 0::2] | (c[..., 1::2] << 4)
    return np.ascontiguousarray(words), np.ascontiguousarray(byte.astype(np.uint8).reshape(k // 512, 16, n))


def unpack_weight(words, scales, fmt):
    g, p, n, _ = words.shape
    if fmt == "e4m3":
        vals = np.ascontiguousarray(words).view(ml_dtypes.float8_e4m3fn).astype(np.float64)
    else:
        nib = np.empty((g, p, n, 4), np.uint8)
        nib[..., 0::2] = words & 0xF
        nib[..., 1::2] = words >> 4
        vals = E2M1[nib]
    vals = vals * np.repeat(np.exp2(scales.astype(np.float64) - 127.0), 8, axis=1)[..., None]
    return vals.transpose(0, 1, 3, 2).reshape(g * 512, n)
def pack4(w):
    words, scales = pack_weight(w, "e2m1")
    return words.reshape(words.shape[0], 128, -1), scales


def unpack4(words, scales):
    return unpack_weight(words.reshape(words.shape[0], 128, -1, 2), scales, "e2m1")


M, K, L, G = 1024, 2048, 1024, 1024


def setup_inputs():
    s = mx_kscale(M)
    t = mx_kscale(K)
    u = mx_kscale(L)
    B = np.random.standard_normal((K, L)) / np.sqrt(2 * K) * t[:, None]
    D = np.random.standard_normal((L, M)) / np.sqrt(L) / u[:, None]
    b_words, b_scales = pack4(B)
    d_words, d_scales = pack4(D)
    return {"x": bf(np.random.standard_normal((M, G)) / s[:, None]),
            "y": bf(np.random.standard_normal((K, G)) / t[:, None]),
            "a": bf(np.random.standard_normal((L, M)) / np.sqrt(2 * M) * s),
            "b_words": b_words, "b_scales": b_scales,
            "r": bf((1 + 0.1 * np.random.standard_normal(L)) * u),
            "d_words": d_words, "d_scales": d_scales,
            "mu": bf(0.5 * np.random.standard_normal(G)),
            "lib": bf(1 + 0.1 * np.random.standard_normal(M))}


def reference(x, y, a, b_words, b_scales, r, d_words, d_scales, mu, lib):
    B = unpack4(b_words, b_scales)
    D = unpack4(d_words, d_scales)
    new = mxq(f64(a), 1, "e4m3") @ mxq(f64(x), 0, "e4m3")
    atlas = B.T @ mxq(f64(y), 0, "e4m3")
    h = (new + atlas) * f64(r)[:, None]
    z = D.T @ mxq(h, 0, "e4m3")
    return (z + f64(mu)[None, :]) * f64(lib)[:, None]

@@ -1,0 +1,309 @@
+from contextlib import ExitStack
+
+import concourse.mybir as mybir
+from concourse.masks import make_identity
+
+M, K, L, G_ALL = 1024, 2048, 1024, 1024
+FLOPS = 2 * L * G_ALL * (M + K) + 2 * M * G_ALL * L
+
+F32 = mybir.dt.float32
+BF16 = mybir.dt.bfloat16
+I32 = mybir.dt.int32
+U32 = mybir.dt.uint32
+U8 = mybir.dt.uint8
+FP8X4 = mybir.dt.float8_e4m3fn_x4
+FP4X4 = mybir.dt.float4_e2m1fn_x4
+MULT = mybir.AluOpType.mult
+ADD = mybir.AluOpType.add
+COPY = mybir.ActivationFunctionType.Copy
+
+P = 128
+W = 512
+V, S = "vector", "scalar"
+FIRST = (0, 0)
+LAST = (5, 5)
+
+
+def tile_magic_landmark_imputation_s3_kernel(tc, x, y, a, b_words, b_scales, r, d_words, d_scales, mu, lib, out):
+    nc = tc.nc
+    with ExitStack() as ctx:
+        keep = ctx.enter_context(tc.tile_pool(name="keep", bufs=1))
+        psum = ctx.enter_context(tc.psum_pool(name="psum", bufs=1))
+        ctx.enter_context(tc.manual_schedule())
+        t = {}
+
+        def sb(key, shape, dtype, tag=None):
+            if key not in t:
+                name = "%s%d" % (key[0], len(t))
+                t[key] = keep.tile(shape, dtype, name=name, tag=tag or name, align_bytes=64)
+            return t[key]
+
+        def bank_tile(key, bank, dtype=F32, width=W):
+            t[key] = psum.tile([P, width], dtype, name="%s%d" % (key[0], len(t)), tag="bank%d" % bank)
+            return t[key]
+
+        def copy(engine, out, in_):
+            if engine == V:
+                nc.vector.tensor_copy(out=out, in_=in_)
+            else:
+                nc.scalar.copy(out=out, in_=in_)
+
+        def quantize(key, source, first, count):
+            codes = sb(("codes",) + key, [P, W], U32)
+            scales = sb(("scales",) + key, [P, W], U8)
+            cols = slice(first, first + count)
+            nc.vector.quantize_mx(out=codes[:, cols].bitcast(FP8X4), scales=scales[:, cols], in_=source[:, 4 * first : 4 * (first + count)])
+
+        def prologue(n):
+            make_identity(nc, sb(("ident32",), [P, P], F32)[:])
+            make_identity(nc, sb(("ident16",), [P, P], BF16)[:])
+            ones = sb(("ones",), [P, W], BF16)
+            nc.vector.memset(ones[:], 1.0)
+            nc.vector.memset(sb(("lib_rows",), [P, P], BF16)[:], 0.0)
+            quantize(("ones",), ones, 0, P)
+            nc.vector.memset(sb(("b_plane",), [P, 4 * L], U8)[:].bitcast(I32), 0)
+            nc.vector.memset(sb(("d_plane",), [P, 2 * M], U8)[:].bitcast(I32), 0)
+            nc.scalar.dma_start(out=sb(("r_raw",), [P, 2, 4], BF16)[:], in_=r.rearrange("(g p w) -> p g w", g=2, w=4))
+            nc.scalar.dma_start(out=sb(("mu_raw",), [P, 8], BF16)[:], in_=mu.rearrange("(p w) -> p w", w=8))
+            nc.scalar.dma_start(out=t["lib_rows",][0:8, :], in_=lib.rearrange("(j p) -> j p", p=P))
+            nc.scalar.activation(out=sb(("unused",), [P, 1], F32)[:], in_=ones[:, 0:1], func=COPY, scale=2.0)
+
+        def warm_up(n):
+            bank = bank_tile(("warm", len(t)), 0)
+            codes, scales = t["codes", "ones"][:, :P].bitcast(FP8X4), t["scales", "ones"][:, :P]
+            for i in range(n):
+                nc.tensor.matmul_mx(out=bank[:, (i % 4) * P : (i % 4 + 1) * P], lhsT=codes, lhsT_scale=scales, rhs=codes, rhs_scale=scales, start=True, stop=True)
+
+        def spread_constants():
+            r_words = t["r_raw",][:].rearrange("p g w -> p (g w)").bitcast(F32)
+            mu_words = t["mu_raw",][:].bitcast(F32)
+            for name, words, bank in (("r", r_words, 1), ("mu", mu_words, 2)):
+                spread = bank_tile(("spread", name), bank)
+                for j in range(4):
+                    nc.tensor.transpose(spread[:, j * P : (j + 1) * P], words[:, j : j + 1].to_broadcast([P, P]), t["ident32",][:])
+            nc.tensor.transpose(bank_tile(("spread", "lib"), 3, BF16, P)[:], t["lib_rows",][:], t["ident16",][:])
+
+        def keep_constants():
+            nc.vector.tensor_copy(out=sb(("r",), [P, L], BF16)[:].bitcast(F32), in_=t["spread", "r"][:])
+            nc.vector.tensor_copy(
+                out=sb(("mu",), [P, G_ALL], BF16)[:].bitcast(F32).rearrange("p (n j) -> p n j", j=4),
+                in_=t["spread", "mu"][:].rearrange("p (j n) -> p n j", j=4),
+            )
+            nc.vector.tensor_copy(out=sb(("lib",), [P, 8], F32)[:], in_=t["spread", "lib"][:, 0:8])
+
+        def load_a(G, c, jp):
+            rows = a[W * G + 256 * jp : W * G + 256 * (jp + 1), W * c : W * (c + 1)]
+            nc.sync.dma_start(out=sb(("a_raw", G, c, jp), [P, 2, W], BF16)[:], in_=rows.rearrange("(j p) k -> p j k", p=P))
+
+        def load_act(c, h):
+            source, first = (x, W * c) if c < 2 else (y, W * (c - 2))
+            rows = source[first : first + W, W * h : W * (h + 1)]
+            nc.sync.dma_start(out=sb(("raw", c, h), [P, 4, W], BF16)[:], in_=rows.rearrange("(p t) g -> p t g", t=4))
+
+        def load_b(k):
+            nc.sync.dma_start(out=sb(("b", k), [P, 2 * L], U8)[:].bitcast(I32), in_=b_words[k].bitcast(I32))
+
+        def load_scales(plane, scales, groups):
+            for q in range(4):
+                nc.sync.dma_start(
+                    out=plane[32 * q : 32 * q + 4, :].bitcast(I32).rearrange("r (g n) -> r g n", g=groups),
+                    in_=scales[:, 4 * q : 4 * q + 4, :].bitcast(I32).rearrange("g r n -> r g n"),
+                )
+
+        def load_b_scales():
+            load_scales(t["b_plane",], b_scales, 4)
+
+        def load_d():
+            load_scales(t["d_plane",], d_scales, 2)
+            nc.sync.dma_start(
+                out=sb(("d",), [P, 4 * M], U8)[:].bitcast(I32).rearrange("p (g n) -> p g n", g=2),
+                in_=d_words.bitcast(I32).rearrange("g p n -> p g n"),
+            )
+
+        def turn_a(G, c, jp, bank):
+            turned = bank_tile(("a_turned", G, c, jp), bank)
+            words = t["a_raw", G, c, jp][:].rearrange("p j k -> p (j k)").bitcast(F32)
+            for j in range(2):
+                for u in range(2):
+                    slot = 2 * j + u
+                    nc.tensor.transpose(turned[:, slot * P : (slot + 1) * P], words[:, 256 * j + u : 256 * (j + 1) : 2], t["ident32",][:])
+
+        def unturn(engine, woven, first, count, turned):
+            words = woven[:].bitcast(F32)[:, 256 * first : 256 * (first + count)]
+            copy(
+                engine,
+                words.rearrange("p (j n u) -> p j n u", j=count, u=2),
+                turned[:, : 256 * count].rearrange("p (j u n) -> p j n u", j=count, u=2),
+            )
+
+        def empty_a(G, c, jp, engine):
+            unturn(engine, sb(("a_woven", G, c), [P, 4 * W], BF16, "a_woven%d" % G), 2 * jp, 2, t["a_turned", G, c, jp])
+
+        def quant_a(G, c, jps):
+            quantize(("a", G, c), t["a_woven", G, c], 256 * jps[0], 256 * len(jps))
+
+        def weave(c, h, half, engine):
+            woven = sb(("woven", c, h), [P, 4 * W], BF16, "woven%d" % c)
+            copy(
+                engine,
+                woven[:, 1024 * half : 1024 * (half + 1)].rearrange("p (c i t) -> p c t i", i=4, t=4),
+                t["raw", c, h][:, :, 256 * half : 256 * (half + 1)].rearrange("p t (c i) -> p c t i", i=4),
+            )
+
+        def quant_act(c, h, halves):
+            quantize(("act", c, h), t["woven", c, h], 256 * halves[0], 256 * len(halves))
+
+        def mm1(h, gt, G, c, bank=None):
+            if bank is not None:
+                bank_tile(("unit", h, gt, G), bank)
+            cols = slice(P * gt, P * (gt + 1))
+            if c < 2:
+                rhs, rhs_scale = t["codes", "a", G, c][:].bitcast(FP8X4), t["scales", "a", G, c][:]
+            else:
+                rhs = t["b", c - 2][:, 2 * W * G : 2 * W * (G + 1)].bitcast(FP4X4)
+                rhs_scale = t["b_plane",][:, L * (c - 2) + W * G : L * (c - 2) + W * (G + 1)]
+            nc.tensor.matmul_mx(
+                out=t["unit", h, gt, G][:],
+                lhsT=t["codes", "act", c, h][:, cols].bitcast(FP8X4),
+                lhsT_scale=t["scales", "act", c, h][:, cols],
+                rhs=rhs,
+                rhs_scale=rhs_scale,
+                start=(c == FIRST[h]),
+                stop=(c == LAST[h]),
+            )
+
+        def empty_unit(h, gt, G):
+            nc.vector.tensor_tensor(
+                out=sb(("ht", h, gt, G), [P, W], BF16)[:].rearrange("g (u p e) -> g u p e", u=2, e=2),
+                in0=t["unit", h, gt, G][:].rearrange("g (p u e) -> g u p e", u=2, e=2),
+                in1=t["r",][:, W * G : W * (G + 1)].rearrange("g (u p e) -> g u p e", u=2, e=2),
+                op=MULT,
+            )
+
+        def turn_h(h, G, gts, bank):
+            turned = bank_tile(("h_turned", h, G, gts), bank)
+            for j, gt in enumerate(gts):
+                words = t["ht", h, gt, G][:].bitcast(F32)
+                for u in range(2):
+                    slot = 2 * j + u
+                    nc.tensor.transpose(turned[:, slot * P : (slot + 1) * P], words[:, u * P : (u + 1) * P], t["ident32",][:])
+
+        def empty_h(h, G, gts, engine):
+            unturn(engine, sb(("h_woven", h, G), [P, 4 * W], BF16, "h_woven%d" % G), gts[0], len(gts), t["h_turned", h, G, gts])
+
+        def quant_h(h, G, gts):
+            quantize(("h", h, G), t["h_woven", h, G], P * gts[0], P * len(gts))
+
+        def scale_mu(h, mt):
+            nc.scalar.activation(out=sb(("o", h, mt), [P, W], F32)[:], in_=t["mu",][:, W * h : W * (h + 1)], func=COPY, scale=t["lib",][:, mt : mt + 1])
+
+        def mm2(h, mt, G, bank=None):
+            if bank is not None:
+                bank_tile(("z", h, mt), bank)
+            nc.tensor.matmul_mx(
+                out=t["z", h, mt][:],
+                lhsT=t["d",][:, 2 * (M * G + P * mt) : 2 * (M * G + P * (mt + 1))].bitcast(FP4X4),
+                lhsT_scale=t["d_plane",][:, M * G + P * mt : M * G + P * (mt + 1)],
+                rhs=t["codes", "h", h, G][:].bitcast(FP8X4),
+                rhs_scale=t["scales", "h", h, G][:],
+                start=(G == 0),
+                stop=(G == 1),
+            )
+
+        def finish(h, mt):
+            o = t["o", h, mt]
+            nc.vector.scalar_tensor_tensor(out=o[:], in0=t["z", h, mt][:], scalar=t["lib",][:, mt : mt + 1], in1=o[:], op0=MULT, op1=ADD)
+            nc.sync.dma_start(out=out[P * mt : P * (mt + 1), W * h : W * (h + 1)], in_=o[:])
+
+        prologue(0)
+        load_a(0, 0, 0); load_a(0, 0, 1); load_act(0, 0)
+        load_a(1, 0, 0); load_a(1, 0, 1); load_a(0, 1, 0); load_a(0, 1, 1); load_act(1, 0)
+        load_a(1, 1, 0); load_a(1, 1, 1)
+        load_b_scales()
+        for k in range(4):
+            load_act(2 + k, 0); load_b(k)
+        for c in range(6):
+            load_act(c, 1)
+        load_d()
+        warm_up(8); spread_constants(); keep_constants()
+        turn_a(0, 0, 0, 6); turn_a(0, 0, 1, 7); empty_a(0, 0, 0, S); empty_a(0, 0, 1, S)
+        warm_up(2)
+        weave(0, 0, 0, V); weave(0, 0, 1, S); quant_a(0, 0, (0, 1)); quant_act(0, 0, (0,))
+        turn_a(1, 0, 0, 4); turn_a(1, 0, 1, 5); empty_a(1, 0, 0, V); quant_act(0, 0, (1,)); empty_a(1, 0, 1, S)
+        for gt in range(4): mm1(0, gt, 0, 0, gt)
+        quant_a(1, 0, (0, 1))
+        scale_mu(0, 0); scale_mu(0, 1)
+        turn_a(0, 1, 0, 6); turn_a(0, 1, 1, 7); empty_a(0, 1, 0, S); empty_a(0, 1, 1, S)
+        weave(1, 0, 0, V)
+        weave(1, 0, 1, V)
+        quant_act(1, 0, (0,))
+        quant_a(0, 1, (0, 1))
+        for gt in range(2): mm1(0, gt, 1, 0, 4 + gt)
+        turn_a(1, 1, 0, 6); turn_a(1, 1, 1, 7); empty_a(1, 1, 0, S); empty_a(1, 1, 1, S)
+        quant_act(1, 0, (1,))
+        for gt in range(4): mm1(0, gt, 0, 1)
+        quant_a(1, 1, (0, 1))
+        for gt in range(2, 4): mm1(0, gt, 1, 0, 4 + gt)
+        for gt in range(4): mm1(0, gt, 1, 1)
+        for c in range(2, 6):
+            weave(c, 0, 0, V); weave(c, 0, 1, S)
+            if c > 3: quant_act(c - 1, 0, (1,))
+            if c in (3, 4):
+                for G in range(2):
+                    for gt in range(4): mm1(0, gt, G, c - 1)
+            quant_act(c, 0, (0,))
+            if c == 2: quant_act(c, 0, (1,))
+            scale_mu(0, c)
+        quant_act(5, 0, (1,))
+        weave(0, 1, 0, S); weave(0, 1, 1, V); weave(1, 1, 0, S); weave(1, 1, 1, S); weave(2, 1, 0, S); weave(2, 1, 1, S)
+        for G in range(2):
+            for gt in range(4):
+                mm1(0, gt, G, 4); mm1(0, gt, G, 5); empty_unit(0, gt, G)
+                if (G, gt) == (0, 0): quant_act(0, 1, (0, 1))
+                if (G, gt) == (0, 3): quant_act(1, 1, (0, 1))
+        quant_act(2, 1, (0, 1))
+        def row(c, units):
+            for G, gt in units: mm1(1, gt, G, c, 4 * G + gt if c == 0 else None)
+        first, second = [(0, gt) for gt in range(4)], [(1, 0), (1, 1)]
+        row(0, first); row(1, first); row(0, second); row(1, second)
+        scale_mu(0, 6)
+        weave(3, 1, 0, V); weave(3, 1, 1, S); weave(4, 1, 0, V); weave(4, 1, 1, S)
+        quant_act(3, 1, (0, 1))
+        turn_h(0, 0, (0, 1), 6); turn_h(0, 0, (2, 3), 7)
+        empty_h(0, 0, (0, 1), V); empty_h(0, 0, (2, 3), S)
+        quant_act(4, 1, (0, 1)); weave(5, 1, 0, V); weave(5, 1, 1, S)
+        row(2, first + second); row(3, first)
+        turn_h(0, 1, (0, 1), 6); turn_h(0, 1, (2, 3), 7)
+        empty_h(0, 1, (0, 1), S); empty_h(0, 1, (2, 3), S)
+        quant_h(0, 0, (0, 1, 2, 3)); quant_act(5, 1, (0, 1)); quant_h(0, 1, (0, 1, 2, 3))
+        scale_mu(0, 7)
+        for mt in range(4): scale_mu(1, mt)
+        row(3, second); row(4, first)
+        zb = (6, 7, 2, 3, 4, 6, 7, 2)
+        def z0(mt):
+            mm2(0, mt, 0, zb[mt]); mm2(0, mt, 1)
+        for gt in range(4):
+            mm1(1, gt, 0, 5); empty_unit(1, gt, 0)
+        for gt in range(2):
+            mm1(1, gt, 1, 4); mm1(1, gt, 1, 5); empty_unit(1, gt, 1)
+        z0(0); z0(1); finish(0, 0); finish(0, 1)
+        def unit(gt, bank):
+            for c in range(6): mm1(1, gt, 1, c, bank if c == 0 else None)
+        turn_h(1, 0, (0, 1), 0); turn_h(1, 0, (2, 3), 1); empty_h(1, 0, (0, 1), S); empty_h(1, 0, (2, 3), S)
+        unit(2, 5); quant_h(1, 0, (0, 1, 2, 3)); empty_unit(1, 2, 1)
+        z0(2); finish(0, 2)
+        turn_h(1, 1, (0, 1), 0); empty_h(1, 1, (0, 1), S)
+        for mt in range(4, 8): scale_mu(1, mt)
+        z0(3); finish(0, 3)
+        unit(3, 1); quant_h(1, 1, (0, 1)); empty_unit(1, 3, 1)
+        z0(4); z0(5)
+        turn_h(1, 1, (2, 3), 0); empty_h(1, 1, (2, 3), S)
+        finish(0, 4); finish(0, 5)
+        z0(6); z0(7)
+        quant_h(1, 1, (2, 3))
+        finish(0, 6); finish(0, 7)
+        order = (3, 5, 1, 4, 6, 0, 7, 2)
+        mm2(1, 0, 0, order[0])
+        for mt in range(8):
+            if mt: mm2(1, mt, 0, order[mt])
+            mm2(1, mt, 1); finish(1, mt)

@@ -55,45 +55,47 @@ def tile_magic_landmark_imputation_s3_kernel(tc, x, y, a, b_words, b_scales, r, 
             nc.vector.quantize_mx(out=codes[:, cols].bitcast(FP8X4), scales=scales[:, cols], in_=source[:, 4 * first : 4 * (first + count)])
 
         def prologue(n):
+            ones = sb(("ones",), [P, W], BF16)
+            nc.gpsimd.memset(ones[:], 1.0)
+            quantize(("ones",), ones, 0, P)
             make_identity(nc, sb(("ident32",), [P, P], F32)[:])
             make_identity(nc, sb(("ident16",), [P, P], BF16)[:])
-            ones = sb(("ones",), [P, W], BF16)
-            nc.vector.memset(ones[:], 1.0)
             nc.vector.memset(sb(("lib_rows",), [P, P], BF16)[:], 0.0)
-            quantize(("ones",), ones, 0, P)
             nc.vector.memset(sb(("b_plane",), [P, 4 * L], U8)[:].bitcast(I32), 0)
             nc.vector.memset(sb(("d_plane",), [P, 2 * M], U8)[:].bitcast(I32), 0)
-            nc.scalar.dma_start(out=sb(("r_raw",), [P, 2, 4], BF16)[:], in_=r.rearrange("(g p w) -> p g w", g=2, w=4))
+            nc.scalar.dma_start(out=sb(("r_raw",), [P, 8], BF16)[:].rearrange("p (g w) -> p g w", g=2), in_=r.rearrange("(g p w) -> p g w", g=2, w=4))
             nc.scalar.dma_start(out=sb(("mu_raw",), [P, 8], BF16)[:], in_=mu.rearrange("(p w) -> p w", w=8))
             nc.scalar.dma_start(out=t["lib_rows",][0:8, :], in_=lib.rearrange("(j p) -> j p", p=P))
             nc.scalar.activation(out=sb(("unused",), [P, 1], F32)[:], in_=ones[:, 0:1], func=COPY, scale=2.0)
 
-        def warm_up(n):
-            bank = bank_tile(("warm", len(t)), 0)
+        def warm_up(n, bank_index):
+            bank = bank_tile(("warm", len(t)), bank_index)
             codes, scales = t["codes", "ones"][:, :P].bitcast(FP8X4), t["scales", "ones"][:, :P]
             for i in range(n):
                 nc.tensor.matmul_mx(out=bank[:, (i % 4) * P : (i % 4 + 1) * P], lhsT=codes, lhsT_scale=scales, rhs=codes, rhs_scale=scales, start=True, stop=True)
 
-        def spread_constants():
-            r_words = t["r_raw",][:].rearrange("p g w -> p (g w)").bitcast(F32)
-            mu_words = t["mu_raw",][:].bitcast(F32)
-            for name, words, bank in (("r", r_words, 1), ("mu", mu_words, 2)):
-                spread = bank_tile(("spread", name), bank)
+        def spread(name, bank):
+            if name == "lib":
+                nc.tensor.transpose(bank_tile(("spread", name), bank, BF16, P)[:], t["lib_rows",][:], t["ident16",][:])
+            else:
+                words = t[name + "_raw",][:].bitcast(F32)
+                turned = bank_tile(("spread", name), bank)
                 for j in range(4):
-                    nc.tensor.transpose(spread[:, j * P : (j + 1) * P], words[:, j : j + 1].to_broadcast([P, P]), t["ident32",][:])
-            nc.tensor.transpose(bank_tile(("spread", "lib"), 3, BF16, P)[:], t["lib_rows",][:], t["ident16",][:])
+                    nc.tensor.transpose(turned[:, j * P : (j + 1) * P], words[:, j : j + 1].to_broadcast([P, P]), t["ident32",][:])
 
-        def keep_constants():
-            nc.vector.tensor_copy(out=sb(("r",), [P, L], BF16)[:].bitcast(F32), in_=t["spread", "r"][:])
-            nc.vector.tensor_copy(
-                out=sb(("mu",), [P, G_ALL], BF16)[:].bitcast(F32).rearrange("p (n j) -> p n j", j=4),
-                in_=t["spread", "mu"][:].rearrange("p (j n) -> p n j", j=4),
-            )
-            nc.vector.tensor_copy(out=sb(("lib",), [P, 8], F32)[:], in_=t["spread", "lib"][:, 0:8])
+        def keep_spread(name, engine):
+            turned = t["spread", name]
+            if name == "lib":
+                copy(engine, sb(("lib",), [P, 8], F32)[:], turned[:, 0:8])
+            elif name == "r":
+                copy(engine, sb(("r",), [P, L], BF16)[:].bitcast(F32), turned[:])
+            else:
+                words = sb(("mu",), [P, G_ALL], BF16)[:].bitcast(F32)
+                copy(engine, words.rearrange("p (n j) -> p n j", j=4), turned[:].rearrange("p (j n) -> p n j", j=4))
 
-        def load_a(G, c, jp):
-            rows = a[W * G + 256 * jp : W * G + 256 * (jp + 1), W * c : W * (c + 1)]
-            nc.sync.dma_start(out=sb(("a_raw", G, c, jp), [P, 2, W], BF16)[:], in_=rows.rearrange("(j p) k -> p j k", p=P))
+        def load_a(G, jp):
+            rows = a[W * G + 256 * jp : W * G + 256 * (jp + 1), :]
+            nc.sync.dma_start(out=sb(("a_raw", G, jp), [P, 2, M], BF16)[:], in_=rows.rearrange("(j p) k -> p j k", p=P))
 
         def load_act(c, h):
             source, first = (x, W * c) if c < 2 else (y, W * (c - 2))
@@ -122,11 +124,11 @@ def tile_magic_landmark_imputation_s3_kernel(tc, x, y, a, b_words, b_scales, r, 
 
         def turn_a(G, c, jp, bank):
             turned = bank_tile(("a_turned", G, c, jp), bank)
-            words = t["a_raw", G, c, jp][:].rearrange("p j k -> p (j k)").bitcast(F32)
+            words = t["a_raw", G, jp][:].rearrange("p j k -> p (j k)").bitcast(F32)
             for j in range(2):
                 for u in range(2):
                     slot = 2 * j + u
-                    nc.tensor.transpose(turned[:, slot * P : (slot + 1) * P], words[:, 256 * j + u : 256 * (j + 1) : 2], t["ident32",][:])
+                    nc.tensor.transpose(turned[:, slot * P : (slot + 1) * P], words[:, W * j + 256 * c + u : W * j + 256 * (c + 1) : 2], t["ident32",][:])
 
         def unturn(engine, woven, first, count, turned):
             words = woven[:].bitcast(F32)[:, 256 * first : 256 * (first + count)]
@@ -137,7 +139,7 @@ def tile_magic_landmark_imputation_s3_kernel(tc, x, y, a, b_words, b_scales, r, 
             )
 
         def empty_a(G, c, jp, engine):
-            unturn(engine, sb(("a_woven", G, c), [P, 4 * W], BF16, "a_woven%d" % G), 2 * jp, 2, t["a_turned", G, c, jp])
+            unturn(engine, sb(("a_woven", G, c), [P, 4 * W], BF16), 2 * jp, 2, t["a_turned", G, c, jp])
 
         def quant_a(G, c, jps):
             quantize(("a", G, c), t["a_woven", G, c], 256 * jps[0], 256 * len(jps))
@@ -174,7 +176,7 @@ def tile_magic_landmark_imputation_s3_kernel(tc, x, y, a, b_words, b_scales, r, 
 
         def empty_unit(h, gt, G):
             nc.vector.tensor_tensor(
-                out=sb(("ht", h, gt, G), [P, W], BF16)[:].rearrange("g (u p e) -> g u p e", u=2, e=2),
+                out=sb(("ht", h, gt, G), [P, W], BF16, "ht%d_%d" % (gt, G))[:].rearrange("g (u p e) -> g u p e", u=2, e=2),
                 in0=t["unit", h, gt, G][:].rearrange("g (p u e) -> g u p e", u=2, e=2),
                 in1=t["r",][:, W * G : W * (G + 1)].rearrange("g (u p e) -> g u p e", u=2, e=2),
                 op=MULT,
@@ -210,40 +212,37 @@ def tile_magic_landmark_imputation_s3_kernel(tc, x, y, a, b_words, b_scales, r, 
                 stop=(G == 1),
             )
 
-        def finish(h, mt):
-            o = t["o", h, mt]
-            nc.vector.scalar_tensor_tensor(out=o[:], in0=t["z", h, mt][:], scalar=t["lib",][:, mt : mt + 1], in1=o[:], op0=MULT, op1=ADD)
-            nc.sync.dma_start(out=out[P * mt : P * (mt + 1), W * h : W * (h + 1)], in_=o[:])
+        def finish(h, mt, pieces=1):
+            width = W // pieces
+            for first in range(0, W, width):
+                o = t["o", h, mt][:, first : first + width]
+                z = t["z", h, mt][:, first : first + width]
+                nc.vector.scalar_tensor_tensor(out=o, in0=z, scalar=t["lib",][:, mt : mt + 1], in1=o, op0=MULT, op1=ADD)
+                nc.sync.dma_start(out=out[P * mt : P * (mt + 1), W * h + first : W * h + first + width], in_=o)
 
         prologue(0)
-        load_a(0, 0, 0); load_a(0, 0, 1); load_act(0, 0)
-        load_a(1, 0, 0); load_a(1, 0, 1); load_a(0, 1, 0); load_a(0, 1, 1); load_act(1, 0)
-        load_a(1, 1, 0); load_a(1, 1, 1)
+        load_a(0, 0); load_a(0, 1); load_act(0, 0); load_a(1, 0); load_a(1, 1); load_act(1, 0)
         load_b_scales()
         for k in range(4):
             load_act(2 + k, 0); load_b(k)
         for c in range(6):
             load_act(c, 1)
         load_d()
-        warm_up(8); spread_constants(); keep_constants()
-        turn_a(0, 0, 0, 6); turn_a(0, 0, 1, 7); empty_a(0, 0, 0, S); empty_a(0, 0, 1, S)
-        warm_up(2)
-        weave(0, 0, 0, V); weave(0, 0, 1, S); quant_a(0, 0, (0, 1)); quant_act(0, 0, (0,))
-        turn_a(1, 0, 0, 4); turn_a(1, 0, 1, 5); empty_a(1, 0, 0, V); quant_act(0, 0, (1,)); empty_a(1, 0, 1, S)
+        warm_up(14, 3)
+        spread("r", 0); spread("mu", 1); spread("lib", 2); keep_spread("lib", V); keep_spread("r", V); keep_spread("mu", V)
+        turn_a(0, 0, 0, 4); turn_a(0, 1, 0, 5); empty_a(0, 0, 0, S); empty_a(0, 1, 0, S)
+        warm_up(8, 3)
+        turn_a(0, 0, 1, 6); turn_a(0, 1, 1, 7); empty_a(0, 0, 1, S); empty_a(0, 1, 1, S)
+        warm_up(6, 3)
+        quant_a(0, 0, (0,)); weave(0, 0, 0, V); weave(0, 0, 1, V); quant_act(0, 0, (0,)); quant_a(0, 0, (1,)); quant_act(0, 0, (1,)); quant_a(0, 1, (0, 1))
+        turn_a(1, 0, 0, 4); turn_a(1, 1, 0, 5); empty_a(1, 0, 0, S); empty_a(1, 1, 0, S)
+        weave(1, 0, 1, S)
         for gt in range(4): mm1(0, gt, 0, 0, gt)
-        quant_a(1, 0, (0, 1))
-        scale_mu(0, 0); scale_mu(0, 1)
-        turn_a(0, 1, 0, 6); turn_a(0, 1, 1, 7); empty_a(0, 1, 0, S); empty_a(0, 1, 1, S)
-        weave(1, 0, 0, V)
-        weave(1, 0, 1, V)
-        quant_act(1, 0, (0,))
-        quant_a(0, 1, (0, 1))
-        for gt in range(2): mm1(0, gt, 1, 0, 4 + gt)
-        turn_a(1, 1, 0, 6); turn_a(1, 1, 1, 7); empty_a(1, 1, 0, S); empty_a(1, 1, 1, S)
-        quant_act(1, 0, (1,))
-        for gt in range(4): mm1(0, gt, 0, 1)
+        turn_a(1, 0, 1, 6); turn_a(1, 1, 1, 7); empty_a(1, 0, 1, S); empty_a(1, 1, 1, S)
+        weave(1, 0, 0, V); quant_a(1, 0, (0,)); quant_act(1, 0, (0,)); quant_act(1, 0, (1,)); quant_a(1, 0, (1,))
         quant_a(1, 1, (0, 1))
-        for gt in range(2, 4): mm1(0, gt, 1, 0, 4 + gt)
+        for gt in range(4): mm1(0, gt, 0, 1)
+        for gt in range(4): mm1(0, gt, 1, 0, 4 + gt)
         for gt in range(4): mm1(0, gt, 1, 1)
         for c in range(2, 6):
             weave(c, 0, 0, V); weave(c, 0, 1, S)
@@ -276,8 +275,8 @@ def tile_magic_landmark_imputation_s3_kernel(tc, x, y, a, b_words, b_scales, r, 
         turn_h(0, 1, (0, 1), 6); turn_h(0, 1, (2, 3), 7)
         empty_h(0, 1, (0, 1), S); empty_h(0, 1, (2, 3), S)
         quant_h(0, 0, (0, 1, 2, 3)); quant_act(5, 1, (0, 1)); quant_h(0, 1, (0, 1, 2, 3))
-        scale_mu(0, 7)
-        for mt in range(4): scale_mu(1, mt)
+        scale_mu(0, 0); scale_mu(0, 1); scale_mu(0, 7)
+        for mt in range(2): scale_mu(1, mt)
         row(3, second); row(4, first)
         zb = (6, 7, 2, 3, 4, 6, 7, 2)
         def z0(mt):
@@ -290,6 +289,7 @@ def tile_magic_landmark_imputation_s3_kernel(tc, x, y, a, b_words, b_scales, r, 
         def unit(gt, bank):
             for c in range(6): mm1(1, gt, 1, c, bank if c == 0 else None)
         turn_h(1, 0, (0, 1), 0); turn_h(1, 0, (2, 3), 1); empty_h(1, 0, (0, 1), S); empty_h(1, 0, (2, 3), S)
+        scale_mu(1, 2); scale_mu(1, 3)
         unit(2, 5); quant_h(1, 0, (0, 1, 2, 3)); empty_unit(1, 2, 1)
         z0(2); finish(0, 2)
         turn_h(1, 1, (0, 1), 0); empty_h(1, 1, (0, 1), S)
@@ -306,4 +306,4 @@ def tile_magic_landmark_imputation_s3_kernel(tc, x, y, a, b_words, b_scales, r, 
         mm2(1, 0, 0, order[0])
         for mt in range(8):
             if mt: mm2(1, mt, 0, order[mt])
-            mm2(1, mt, 1); finish(1, mt)
+            mm2(1, mt, 1); finish(1, mt, 2 if mt == 7 else 1)

@@ -55,12 +55,12 @@ def tile_magic_landmark_imputation_s3_kernel(tc, x, y, a, b_words, b_scales, r, 
             nc.vector.quantize_mx(out=codes[:, cols].bitcast(FP8X4), scales=scales[:, cols], in_=source[:, 4 * first : 4 * (first + count)])
 
         def prologue(n):
+            nc.gpsimd.memset(sb(("lib_rows",), [P, P], BF16)[:], 0.0)
             ones = sb(("ones",), [P, W], BF16)
             nc.gpsimd.memset(ones[:], 1.0)
             quantize(("ones",), ones, 0, P)
             make_identity(nc, sb(("ident32",), [P, P], F32)[:])
             make_identity(nc, sb(("ident16",), [P, P], BF16)[:])
-            nc.vector.memset(sb(("lib_rows",), [P, P], BF16)[:], 0.0)
             nc.vector.memset(sb(("b_plane",), [P, 4 * L], U8)[:].bitcast(I32), 0)
             nc.vector.memset(sb(("d_plane",), [P, 2 * M], U8)[:].bitcast(I32), 0)
             nc.scalar.dma_start(out=sb(("r_raw",), [P, 8], BF16)[:].rearrange("p (g w) -> p g w", g=2), in_=r.rearrange("(g p w) -> p g w", g=2, w=4))
@@ -106,11 +106,9 @@ def tile_magic_landmark_imputation_s3_kernel(tc, x, y, a, b_words, b_scales, r, 
             nc.sync.dma_start(out=sb(("b", k), [P, 2 * L], U8)[:].bitcast(I32), in_=b_words[k].bitcast(I32))
 
         def load_scales(plane, scales, groups):
-            for q in range(4):
-                nc.sync.dma_start(
-                    out=plane[32 * q : 32 * q + 4, :].bitcast(I32).rearrange("r (g n) -> r g n", g=groups),
-                    in_=scales[:, 4 * q : 4 * q + 4, :].bitcast(I32).rearrange("g r n -> r g n"),
-                )
+            rows = scales.bitcast(I32).rearrange("g (q r) n -> r q g n", r=4)
+            for r in range(4):
+                nc.sync.dma_start(out=plane[r:P:32, :].bitcast(I32).rearrange("q (g n) -> q g n", g=groups), in_=rows[r])
 
         def load_b_scales():
             load_scales(t["b_plane",], b_scales, 4)
@@ -221,26 +219,28 @@ def tile_magic_landmark_imputation_s3_kernel(tc, x, y, a, b_words, b_scales, r, 
                 nc.sync.dma_start(out=out[P * mt : P * (mt + 1), W * h + first : W * h + first + width], in_=o)
 
         prologue(0)
-        load_a(0, 0); load_a(0, 1); load_act(0, 0); load_a(1, 0); load_a(1, 1); load_act(1, 0)
+        load_a(0, 0); load_act(0, 0); load_a(0, 1); load_a(1, 0); load_act(1, 0); load_a(1, 1)
         load_b_scales()
         for k in range(4):
             load_act(2 + k, 0); load_b(k)
         for c in range(6):
             load_act(c, 1)
         load_d()
-        warm_up(14, 3)
-        spread("r", 0); spread("mu", 1); spread("lib", 2); keep_spread("lib", V); keep_spread("r", V); keep_spread("mu", V)
+        warm_up(15, 3)
         turn_a(0, 0, 0, 4); turn_a(0, 1, 0, 5); empty_a(0, 0, 0, S); empty_a(0, 1, 0, S)
-        warm_up(8, 3)
-        turn_a(0, 0, 1, 6); turn_a(0, 1, 1, 7); empty_a(0, 0, 1, S); empty_a(0, 1, 1, S)
-        warm_up(6, 3)
-        quant_a(0, 0, (0,)); weave(0, 0, 0, V); weave(0, 0, 1, V); quant_act(0, 0, (0,)); quant_a(0, 0, (1,)); quant_act(0, 0, (1,)); quant_a(0, 1, (0, 1))
+        warm_up(3, 3)
+        spread("r", 0); spread("mu", 1); spread("lib", 2)
+        warm_up(4, 3)
+        weave(0, 0, 0, V); weave(0, 0, 1, V); quant_act(0, 0, (0,)); quant_a(0, 0, (0,)); quant_act(0, 0, (1,))
+        keep_spread("r", S); keep_spread("lib", V)
+        turn_a(0, 0, 1, 6); turn_a(0, 1, 1, 7); empty_a(0, 0, 1, S); keep_spread("mu", V); empty_a(0, 1, 1, S)
+        quant_a(0, 0, (1,))
         turn_a(1, 0, 0, 4); turn_a(1, 1, 0, 5); empty_a(1, 0, 0, S); empty_a(1, 1, 0, S)
-        weave(1, 0, 1, S)
         for gt in range(4): mm1(0, gt, 0, 0, gt)
+        quant_a(0, 1, (0, 1))
+        weave(1, 0, 0, V); weave(1, 0, 1, V); quant_act(1, 0, (0,)); quant_a(1, 0, (0,)); quant_act(1, 0, (1,)); quant_a(1, 1, (0,))
         turn_a(1, 0, 1, 6); turn_a(1, 1, 1, 7); empty_a(1, 0, 1, S); empty_a(1, 1, 1, S)
-        weave(1, 0, 0, V); quant_a(1, 0, (0,)); quant_act(1, 0, (0,)); quant_act(1, 0, (1,)); quant_a(1, 0, (1,))
-        quant_a(1, 1, (0, 1))
+        quant_a(1, 0, (1,)); quant_a(1, 1, (1,))
         for gt in range(4): mm1(0, gt, 0, 1)
         for gt in range(4): mm1(0, gt, 1, 0, 4 + gt)
         for gt in range(4): mm1(0, gt, 1, 1)
@@ -248,37 +248,40 @@ def tile_magic_landmark_imputation_s3_kernel(tc, x, y, a, b_words, b_scales, r, 
             weave(c, 0, 0, V); weave(c, 0, 1, S)
             if c > 3: quant_act(c - 1, 0, (1,))
             if c in (3, 4):
-                for G in range(2):
-                    for gt in range(4): mm1(0, gt, G, c - 1)
+                for gt in range(4):
+                    for G in range(2): mm1(0, gt, G, c - 1)
             quant_act(c, 0, (0,))
             if c == 2: quant_act(c, 0, (1,))
-            scale_mu(0, c)
+            scale_mu(0, c - 2)
         quant_act(5, 0, (1,))
-        weave(0, 1, 0, S); weave(0, 1, 1, V); weave(1, 1, 0, S); weave(1, 1, 1, S); weave(2, 1, 0, S); weave(2, 1, 1, S)
+        weave(0, 1, 0, S); weave(1, 1, 0, S); weave(2, 1, 0, S); weave(2, 1, 1, S); weave(3, 1, 0, S); weave(3, 1, 1, S)
+        for gt in range(2): mm1(0, gt, 0, 4)
         for G in range(2):
             for gt in range(4):
-                mm1(0, gt, G, 4); mm1(0, gt, G, 5); empty_unit(0, gt, G)
-                if (G, gt) == (0, 0): quant_act(0, 1, (0, 1))
-                if (G, gt) == (0, 3): quant_act(1, 1, (0, 1))
-        quant_act(2, 1, (0, 1))
+                if 4 * G + gt >= 2: mm1(0, gt, G, 4)
+                mm1(0, gt, G, 5); empty_unit(0, gt, G)
+                if (G, gt) == (0, 0): weave(0, 1, 1, V); weave(1, 1, 1, V); quant_act(0, 1, (0, 1))
+                if (G, gt) == (0, 1): quant_act(1, 1, (0, 1))
+                if (G, gt) == (1, 1): quant_act(2, 1, (0, 1))
         def row(c, units):
             for G, gt in units: mm1(1, gt, G, c, 4 * G + gt if c == 0 else None)
         first, second = [(0, gt) for gt in range(4)], [(1, 0), (1, 1)]
-        row(0, first); row(1, first); row(0, second); row(1, second)
-        scale_mu(0, 6)
-        weave(3, 1, 0, V); weave(3, 1, 1, S); weave(4, 1, 0, V); weave(4, 1, 1, S)
-        quant_act(3, 1, (0, 1))
+        both = [(0, 0), (1, 0), (0, 1), (1, 1), (0, 2), (0, 3)]
+        for pair in (first[:2], first[2:], second):
+            row(0, pair); row(1, pair)
+        quant_act(3, 1, (0, 1)); weave(4, 1, 0, V); weave(4, 1, 1, S); weave(5, 1, 0, V); weave(5, 1, 1, S); quant_act(4, 1, (0, 1))
+        row(2, both)
         turn_h(0, 0, (0, 1), 6); turn_h(0, 0, (2, 3), 7)
-        empty_h(0, 0, (0, 1), V); empty_h(0, 0, (2, 3), S)
-        quant_act(4, 1, (0, 1)); weave(5, 1, 0, V); weave(5, 1, 1, S)
-        row(2, first + second); row(3, first)
+        empty_h(0, 0, (0, 1), V); empty_h(0, 0, (2, 3), S); quant_act(5, 1, (0, 1))
+        row(3, both)
+        scale_mu(0, 4); scale_mu(0, 5)
         turn_h(0, 1, (0, 1), 6); turn_h(0, 1, (2, 3), 7)
         empty_h(0, 1, (0, 1), S); empty_h(0, 1, (2, 3), S)
-        quant_h(0, 0, (0, 1, 2, 3)); quant_act(5, 1, (0, 1)); quant_h(0, 1, (0, 1, 2, 3))
-        scale_mu(0, 0); scale_mu(0, 1); scale_mu(0, 7)
-        for mt in range(2): scale_mu(1, mt)
-        row(3, second); row(4, first)
-        zb = (6, 7, 2, 3, 4, 6, 7, 2)
+        quant_h(0, 0, (0, 1, 2, 3)); quant_h(0, 1, (0, 1, 2, 3))
+        scale_mu(0, 6); scale_mu(0, 7)
+        for mt in range(6): scale_mu(1, mt)
+        row(4, first)
+        zb = (6, 7, 4, 5, 7, 2, 1, 3)
         def z0(mt):
             mm2(0, mt, 0, zb[mt]); mm2(0, mt, 1)
         for gt in range(4):
@@ -288,22 +291,18 @@ def tile_magic_landmark_imputation_s3_kernel(tc, x, y, a, b_words, b_scales, r, 
         z0(0); z0(1); finish(0, 0); finish(0, 1)
         def unit(gt, bank):
             for c in range(6): mm1(1, gt, 1, c, bank if c == 0 else None)
-        turn_h(1, 0, (0, 1), 0); turn_h(1, 0, (2, 3), 1); empty_h(1, 0, (0, 1), S); empty_h(1, 0, (2, 3), S)
-        scale_mu(1, 2); scale_mu(1, 3)
-        unit(2, 5); quant_h(1, 0, (0, 1, 2, 3)); empty_unit(1, 2, 1)
-        z0(2); finish(0, 2)
-        turn_h(1, 1, (0, 1), 0); empty_h(1, 1, (0, 1), S)
-        for mt in range(4, 8): scale_mu(1, mt)
-        z0(3); finish(0, 3)
-        unit(3, 1); quant_h(1, 1, (0, 1)); empty_unit(1, 3, 1)
+        unit(2, 2); empty_unit(1, 2, 1)
+        turn_h(1, 0, (0, 1), 0); turn_h(1, 0, (2, 3), 1); turn_h(1, 1, (0, 1), 3)
+        empty_h(1, 0, (0, 1), S); empty_h(1, 0, (2, 3), S); empty_h(1, 1, (0, 1), S)
+        scale_mu(1, 6); scale_mu(1, 7)
+        z0(2); z0(3); finish(0, 2); quant_h(1, 0, (0, 1, 2, 3)); finish(0, 3)
+        unit(3, 6); quant_h(1, 1, (0, 1)); empty_unit(1, 3, 1)
         z0(4); z0(5)
         turn_h(1, 1, (2, 3), 0); empty_h(1, 1, (2, 3), S)
         finish(0, 4); finish(0, 5)
         z0(6); z0(7)
         quant_h(1, 1, (2, 3))
         finish(0, 6); finish(0, 7)
-        order = (3, 5, 1, 4, 6, 0, 7, 2)
-        mm2(1, 0, 0, order[0])
+        order = (4, 5, 6, 7, 2, 0, 1, 3)
         for mt in range(8):
-            if mt: mm2(1, mt, 0, order[mt])
-            mm2(1, mt, 1); finish(1, mt, 2 if mt == 7 else 1)
+            mm2(1, mt, 0, order[mt]); mm2(1, mt, 1); finish(1, mt)

@@ -20,8 +20,6 @@ COPY = mybir.ActivationFunctionType.Copy
 P = 128
 W = 512
 V, S = "vector", "scalar"
-FIRST = (0, 0)
-LAST = (5, 5)
 
 
 def tile_magic_landmark_imputation_s3_kernel(tc, x, y, a, b_words, b_scales, r, d_words, d_scales, mu, lib, out):
@@ -66,6 +64,7 @@ def tile_magic_landmark_imputation_s3_kernel(tc, x, y, a, b_words, b_scales, r, 
             nc.scalar.dma_start(out=sb(("r_raw",), [P, 8], BF16)[:].rearrange("p (g w) -> p g w", g=2), in_=r.rearrange("(g p w) -> p g w", g=2, w=4))
             nc.scalar.dma_start(out=sb(("mu_raw",), [P, 8], BF16)[:], in_=mu.rearrange("(p w) -> p w", w=8))
             nc.scalar.dma_start(out=t["lib_rows",][0:8, :], in_=lib.rearrange("(j p) -> j p", p=P))
+            nc.vector.tensor_copy(out=sb(("r_column",), [P, 4], F32)[:], in_=t["r_raw",][:, 0:4])
             nc.scalar.activation(out=sb(("unused",), [P, 1], F32)[:], in_=ones[:, 0:1], func=COPY, scale=2.0)
 
         def warm_up(n, bank_index):
@@ -80,22 +79,25 @@ def tile_magic_landmark_imputation_s3_kernel(tc, x, y, a, b_words, b_scales, r, 
             else:
                 words = t[name + "_raw",][:].bitcast(F32)
                 turned = bank_tile(("spread", name), bank)
-                for j in range(4):
-                    nc.tensor.transpose(turned[:, j * P : (j + 1) * P], words[:, j : j + 1].to_broadcast([P, P]), t["ident32",][:])
+                for slot, j in enumerate(range(2 if name == "r" else 0, 4)):
+                    nc.tensor.transpose(turned[:, slot * P : (slot + 1) * P], words[:, j : j + 1].to_broadcast([P, P]), t["ident32",][:])
 
         def keep_spread(name, engine):
             turned = t["spread", name]
             if name == "lib":
                 copy(engine, sb(("lib",), [P, 8], F32)[:], turned[:, 0:8])
             elif name == "r":
-                copy(engine, sb(("r",), [P, L], BF16)[:].bitcast(F32), turned[:])
+                copy(engine, sb(("r",), [P, W], BF16)[:].bitcast(F32), turned[:, : 2 * P])
             else:
                 words = sb(("mu",), [P, G_ALL], BF16)[:].bitcast(F32)
                 copy(engine, words.rearrange("p (n j) -> p n j", j=4), turned[:].rearrange("p (j n) -> p n j", j=4))
 
         def load_a(G, jp):
-            rows = a[W * G + 256 * jp : W * G + 256 * (jp + 1), :]
-            nc.sync.dma_start(out=sb(("a_raw", G, jp), [P, 2, M], BF16)[:], in_=rows.rearrange("(j p) k -> p j k", p=P))
+            if G == 0:
+                rows = a[:W, :].rearrange("(p t) k -> p t k", t=4)[:, 2 * jp : 2 * jp + 2, :]
+            else:
+                rows = a[W + 256 * jp : W + 256 * (jp + 1), :].rearrange("(j p) k -> p j k", p=P)
+            nc.sync.dma_start(out=sb(("a_raw", G, jp), [P, 2, M], BF16)[:], in_=rows)
 
         def load_act(c, h):
             source, first = (x, W * c) if c < 2 else (y, W * (c - 2))
@@ -142,48 +144,73 @@ def tile_magic_landmark_imputation_s3_kernel(tc, x, y, a, b_words, b_scales, r, 
         def quant_a(G, c, jps):
             quantize(("a", G, c), t["a_woven", G, c], 256 * jps[0], 256 * len(jps))
 
-        def weave(c, h, half, engine):
-            woven = sb(("woven", c, h), [P, 4 * W], BF16, "woven%d" % c)
+        def interleave(engine, woven, rows, half):
             copy(
                 engine,
                 woven[:, 1024 * half : 1024 * (half + 1)].rearrange("p (c i t) -> p c t i", i=4, t=4),
-                t["raw", c, h][:, :, 256 * half : 256 * (half + 1)].rearrange("p t (c i) -> p c t i", i=4),
+                rows[:, :, 256 * half : 256 * (half + 1)].rearrange("p t (c i) -> p c t i", i=4),
             )
+
+        def weave(c, h, half, engine):
+            interleave(engine, sb(("woven", c, h), [P, 4 * W], BF16, "woven%d" % c), t["raw", c, h], half)
+
+        def weave_h(h, half, engine):
+            interleave(engine, sb(("h_woven", h, 0), [P, 4 * W], BF16, "h_woven0"), t["h_rows", h], half)
 
         def quant_act(c, h, halves):
             quantize(("act", c, h), t["woven", c, h], 256 * halves[0], 256 * len(halves))
 
-        def mm1(h, gt, G, c, bank=None):
-            if bank is not None:
-                bank_tile(("unit", h, gt, G), bank)
-            cols = slice(P * gt, P * (gt + 1))
-            if c < 2:
-                rhs, rhs_scale = t["codes", "a", G, c][:].bitcast(FP8X4), t["scales", "a", G, c][:]
-            else:
-                rhs = t["b", c - 2][:, 2 * W * G : 2 * W * (G + 1)].bitcast(FP4X4)
-                rhs_scale = t["b_plane",][:, L * (c - 2) + W * G : L * (c - 2) + W * (G + 1)]
-            nc.tensor.matmul_mx(
-                out=t["unit", h, gt, G][:],
-                lhsT=t["codes", "act", c, h][:, cols].bitcast(FP8X4),
-                lhsT_scale=t["scales", "act", c, h][:, cols],
-                rhs=rhs,
-                rhs_scale=rhs_scale,
-                start=(c == FIRST[h]),
-                stop=(c == LAST[h]),
+        def sort_b(k):
+            nc.vector.tensor_copy(
+                out=sb(("b_sorted", k), [P, 2 * W], U8)[:].rearrange("p (t m b) -> p t m b", t=4, b=2),
+                in_=t["b", k][:, : 2 * W].rearrange("p (m t b) -> p t m b", t=4, b=2),
             )
 
-        def empty_unit(h, gt, G):
-            nc.vector.tensor_tensor(
-                out=sb(("ht", h, gt, G), [P, W], BF16, "ht%d_%d" % (gt, G))[:].rearrange("g (u p e) -> g u p e", u=2, e=2),
-                in0=t["unit", h, gt, G][:].rearrange("g (p u e) -> g u p e", u=2, e=2),
-                in1=t["r",][:, W * G : W * (G + 1)].rearrange("g (u p e) -> g u p e", u=2, e=2),
-                op=MULT,
+        def sort_scales(k):
+            nc.vector.tensor_copy(
+                out=sb(("b_scales_sorted", k), [P, W], U8)[:].rearrange("p (t m) -> p t m", t=4),
+                in_=t["b_plane",][:, L * k : L * k + W].rearrange("p (m t) -> p t m", t=4),
             )
+
+        def mm1(h, j, G, c, bank=None):
+            if bank is not None:
+                bank_tile(("unit", h, j, G), bank)
+            cols = slice(P * j, P * (j + 1)) if G == 1 else slice(0, W)
+            genes = (t["codes", "act", c, h][:, cols].bitcast(FP8X4), t["scales", "act", c, h][:, cols])
+            cols = slice(P * j, P * (j + 1)) if G == 0 else slice(0, W)
+            if c < 2:
+                marks = (t["codes", "a", G, c][:, cols].bitcast(FP8X4), t["scales", "a", G, c][:, cols])
+            elif G == 0:
+                marks = (t["b_sorted", c - 2][:, 2 * cols.start : 2 * cols.stop].bitcast(FP4X4), t["b_scales_sorted", c - 2][:, cols])
+            else:
+                marks = (t["b", c - 2][:, 2 * W :].bitcast(FP4X4), t["b_plane",][:, L * (c - 2) + W : L * (c - 1)])
+            still, moving = (marks, genes) if G == 0 else (genes, marks)
+            nc.tensor.matmul_mx(
+                out=t["unit", h, j, G][:],
+                lhsT=still[0],
+                lhsT_scale=still[1],
+                rhs=moving[0],
+                rhs_scale=moving[1],
+                start=(c == 0),
+                stop=(c == 5),
+            )
+
+        def empty_unit(h, j, G):
+            if G == 0:
+                rows = sb(("h_rows", h), [P, 4, W], BF16, "h_rows")
+                nc.scalar.activation(out=rows[:, j, :], in_=t["unit", h, j, G][:], func=COPY, scale=t["r_column",][:, j : j + 1])
+            else:
+                nc.vector.tensor_tensor(
+                    out=sb(("ht", h, j), [P, W], BF16, "ht%d" % j)[:].rearrange("g (u p e) -> g u p e", u=2, e=2),
+                    in0=t["unit", h, j, G][:].rearrange("g (p u e) -> g u p e", u=2, e=2),
+                    in1=t["r",][:].rearrange("g (u p e) -> g u p e", u=2, e=2),
+                    op=MULT,
+                )
 
         def turn_h(h, G, gts, bank):
             turned = bank_tile(("h_turned", h, G, gts), bank)
             for j, gt in enumerate(gts):
-                words = t["ht", h, gt, G][:].bitcast(F32)
+                words = t["ht", h, gt][:].bitcast(F32)
                 for u in range(2):
                     slot = 2 * j + u
                     nc.tensor.transpose(turned[:, slot * P : (slot + 1) * P], words[:, u * P : (u + 1) * P], t["ident32",][:])
@@ -222,7 +249,7 @@ def tile_magic_landmark_imputation_s3_kernel(tc, x, y, a, b_words, b_scales, r, 
         load_a(0, 0); load_act(0, 0); load_a(0, 1); load_a(1, 0); load_act(1, 0); load_a(1, 1)
         load_b_scales()
         for k in range(4):
-            load_act(2 + k, 0); load_b(k)
+            load_b(k); load_act(2 + k, 0)
         for c in range(6):
             load_act(c, 1)
         load_d()
@@ -231,78 +258,75 @@ def tile_magic_landmark_imputation_s3_kernel(tc, x, y, a, b_words, b_scales, r, 
         warm_up(3, 3)
         spread("r", 0); spread("mu", 1); spread("lib", 2)
         warm_up(4, 3)
-        weave(0, 0, 0, V); weave(0, 0, 1, V); quant_act(0, 0, (0,)); quant_a(0, 0, (0,)); quant_act(0, 0, (1,))
+        weave(0, 0, 0, V); weave(0, 0, 1, V); quant_a(0, 0, (0,)); quant_act(0, 0, (0, 1))
         keep_spread("r", S); keep_spread("lib", V)
-        turn_a(0, 0, 1, 6); turn_a(0, 1, 1, 7); empty_a(0, 0, 1, S); keep_spread("mu", V); empty_a(0, 1, 1, S)
-        quant_a(0, 0, (1,))
+        turn_a(0, 0, 1, 6); turn_a(0, 1, 1, 7); keep_spread("mu", S); empty_a(0, 0, 1, S); empty_a(0, 1, 1, S)
+        quant_a(0, 1, (0,)); quant_a(0, 0, (1,))
+        for j in range(2): mm1(0, j, 0, 0, j)
         turn_a(1, 0, 0, 4); turn_a(1, 1, 0, 5); empty_a(1, 0, 0, S); empty_a(1, 1, 0, S)
-        for gt in range(4): mm1(0, gt, 0, 0, gt)
-        quant_a(0, 1, (0, 1))
-        weave(1, 0, 0, V); weave(1, 0, 1, V); quant_act(1, 0, (0,)); quant_a(1, 0, (0,)); quant_act(1, 0, (1,)); quant_a(1, 1, (0,))
+        for j in range(2, 4): mm1(0, j, 0, 0, j)
+        weave(1, 0, 0, V); quant_a(0, 1, (1,)); weave(1, 0, 1, V); quant_a(1, 0, (0,)); quant_act(1, 0, (0, 1)); quant_a(1, 1, (0,))
         turn_a(1, 0, 1, 6); turn_a(1, 1, 1, 7); empty_a(1, 0, 1, S); empty_a(1, 1, 1, S)
-        quant_a(1, 0, (1,)); quant_a(1, 1, (1,))
-        for gt in range(4): mm1(0, gt, 0, 1)
+        sort_scales(0); quant_a(1, 0, (1,)); sort_b(0); quant_a(1, 1, (1,))
+        for j in range(4): mm1(0, j, 0, 1)
         for gt in range(4): mm1(0, gt, 1, 0, 4 + gt)
         for gt in range(4): mm1(0, gt, 1, 1)
         for c in range(2, 6):
             weave(c, 0, 0, V); weave(c, 0, 1, S)
-            if c > 3: quant_act(c - 1, 0, (1,))
-            if c in (3, 4):
-                for gt in range(4):
-                    for G in range(2): mm1(0, gt, G, c - 1)
-            quant_act(c, 0, (0,))
-            if c == 2: quant_act(c, 0, (1,))
-            scale_mu(0, c - 2)
-        quant_act(5, 0, (1,))
-        weave(0, 1, 0, S); weave(1, 1, 0, S); weave(2, 1, 0, S); weave(2, 1, 1, S); weave(3, 1, 0, S); weave(3, 1, 1, S)
-        for gt in range(2): mm1(0, gt, 0, 4)
-        for G in range(2):
-            for gt in range(4):
-                if 4 * G + gt >= 2: mm1(0, gt, G, 4)
-                mm1(0, gt, G, 5); empty_unit(0, gt, G)
-                if (G, gt) == (0, 0): weave(0, 1, 1, V); weave(1, 1, 1, V); quant_act(0, 1, (0, 1))
-                if (G, gt) == (0, 1): quant_act(1, 1, (0, 1))
-                if (G, gt) == (1, 1): quant_act(2, 1, (0, 1))
+            if c < 5: sort_scales(c - 1)
+            quant_act(c, 0, (0,)); quant_act(c, 0, (1,))
+            if c < 4: sort_b(c - 1)
+            if c < 4:
+                for gt in range(4): mm1(0, gt, 1, c)
+                for j in range(4): mm1(0, j, 0, c)
+            if c < 5: scale_mu(0, c - 2)
+        sort_b(3)
+        order = [(1, 0), (1, 1), (0, 0), (0, 1), (0, 2), (0, 3), (1, 2), (1, 3)]
+        weave(0, 1, 0, V); weave(0, 1, 1, S); weave(1, 1, 1, S)
+        for G, gt in order[:4]: mm1(0, gt, G, 4)
+        for i, (G, gt) in enumerate(order):
+            if i >= 4: mm1(0, gt, G, 4)
+            mm1(0, gt, G, 5); empty_unit(0, gt, G)
+            if i == 0: quant_act(0, 1, (0, 1)); weave(1, 1, 0, V)
+            if i == 1: quant_act(1, 1, (0, 1)); weave(2, 1, 0, V)
+            if i == 5: weave(2, 1, 1, S); weave(3, 1, 1, S)
+            if i == 6: weave(3, 1, 0, V); quant_act(2, 1, (0, 1))
         def row(c, units):
             for G, gt in units: mm1(1, gt, G, c, 4 * G + gt if c == 0 else None)
-        first, second = [(0, gt) for gt in range(4)], [(1, 0), (1, 1)]
-        both = [(0, 0), (1, 0), (0, 1), (1, 1), (0, 2), (0, 3)]
-        for pair in (first[:2], first[2:], second):
-            row(0, pair); row(1, pair)
-        quant_act(3, 1, (0, 1)); weave(4, 1, 0, V); weave(4, 1, 1, S); weave(5, 1, 0, V); weave(5, 1, 1, S); quant_act(4, 1, (0, 1))
-        row(2, both)
-        turn_h(0, 0, (0, 1), 6); turn_h(0, 0, (2, 3), 7)
-        empty_h(0, 0, (0, 1), V); empty_h(0, 0, (2, 3), S); quant_act(5, 1, (0, 1))
-        row(3, both)
-        scale_mu(0, 4); scale_mu(0, 5)
+        six = order[:6]
+        row(0, six); row(1, six)
+        weave(4, 1, 0, V); quant_act(3, 1, (0, 1)); weave(4, 1, 1, S)
+        row(2, six)
         turn_h(0, 1, (0, 1), 6); turn_h(0, 1, (2, 3), 7)
+        weave(5, 1, 0, V); weave(5, 1, 1, S); quant_act(4, 1, (0, 1))
         empty_h(0, 1, (0, 1), S); empty_h(0, 1, (2, 3), S)
-        quant_h(0, 0, (0, 1, 2, 3)); quant_h(0, 1, (0, 1, 2, 3))
-        scale_mu(0, 6); scale_mu(0, 7)
-        for mt in range(6): scale_mu(1, mt)
-        row(4, first)
-        zb = (6, 7, 4, 5, 7, 2, 1, 3)
+        weave_h(0, 0, V); quant_act(5, 1, (0, 1)); weave_h(0, 1, V); quant_h(0, 1, (0, 1, 2, 3)); quant_h(0, 0, (0, 1, 2, 3))
+        row(3, six)
+        for mt in range(3, 8): scale_mu(0, mt)
+        zb = (6, 7, 4, 5, 7, 4, 1, 3)
         def z0(mt):
             mm2(0, mt, 0, zb[mt]); mm2(0, mt, 1)
-        for gt in range(4):
-            mm1(1, gt, 0, 5); empty_unit(1, gt, 0)
-        for gt in range(2):
-            mm1(1, gt, 1, 4); mm1(1, gt, 1, 5); empty_unit(1, gt, 1)
+        for G, gt in [(0, 0), (0, 1), (0, 2), (0, 3), (1, 0), (1, 1)]:
+            mm1(1, gt, G, 4); mm1(1, gt, G, 5); empty_unit(1, gt, G)
         z0(0); z0(1); finish(0, 0); finish(0, 1)
+        weave_h(1, 0, S); weave_h(1, 1, V)
+        for mt in range(4): scale_mu(1, mt)
         def unit(gt, bank):
             for c in range(6): mm1(1, gt, 1, c, bank if c == 0 else None)
         unit(2, 2); empty_unit(1, 2, 1)
-        turn_h(1, 0, (0, 1), 0); turn_h(1, 0, (2, 3), 1); turn_h(1, 1, (0, 1), 3)
-        empty_h(1, 0, (0, 1), S); empty_h(1, 0, (2, 3), S); empty_h(1, 1, (0, 1), S)
-        scale_mu(1, 6); scale_mu(1, 7)
-        z0(2); z0(3); finish(0, 2); quant_h(1, 0, (0, 1, 2, 3)); finish(0, 3)
-        unit(3, 6); quant_h(1, 1, (0, 1)); empty_unit(1, 3, 1)
+        z0(2); z0(3); finish(0, 2); quant_h(1, 0, (0, 1, 2, 3))
+        turn_h(1, 1, (0, 1), 3); turn_h(1, 1, (2,), 1)
+        empty_h(1, 1, (0, 1), S); empty_h(1, 1, (2,), S)
+        for mt in range(4, 6): scale_mu(1, mt)
+        finish(0, 3)
+        unit(3, 6); quant_h(1, 1, (0, 1)); quant_h(1, 1, (2,)); empty_unit(1, 3, 1)
         z0(4); z0(5)
-        turn_h(1, 1, (2, 3), 0); empty_h(1, 1, (2, 3), S)
+        turn_h(1, 1, (3,), 0); empty_h(1, 1, (3,), S)
+        for mt in range(6, 8): scale_mu(1, mt)
         finish(0, 4); finish(0, 5)
         z0(6); z0(7)
-        quant_h(1, 1, (2, 3))
+        quant_h(1, 1, (3,))
         finish(0, 6); finish(0, 7)
-        order = (4, 5, 6, 7, 2, 0, 1, 3)
+        banks = (5, 2, 6, 7, 4, 0, 1, 3)
         for mt in range(8):
-            mm2(1, mt, 0, order[mt]); mm2(1, mt, 1); finish(1, mt)
+            mm2(1, mt, 0, banks[mt]); mm2(1, mt, 1); finish(1, mt)

@@ -30,10 +30,10 @@ def tile_magic_landmark_imputation_s3_kernel(tc, x, y, a, b_words, b_scales, r, 
         ctx.enter_context(tc.manual_schedule())
         t = {}
 
-        def sb(key, shape, dtype, tag=None):
+        def sb(key, shape, dtype, tag=None, align=64):
             if key not in t:
                 name = "%s%d" % (key[0], len(t))
-                t[key] = keep.tile(shape, dtype, name=name, tag=tag or name, align_bytes=64)
+                t[key] = keep.tile(shape, dtype, name=name, tag=tag or name, align_bytes=align)
             return t[key]
 
         def bank_tile(key, bank, dtype=F32, width=W):
@@ -47,8 +47,8 @@ def tile_magic_landmark_imputation_s3_kernel(tc, x, y, a, b_words, b_scales, r, 
                 nc.scalar.copy(out=out, in_=in_)
 
         def quantize(key, source, first, count):
-            codes = sb(("codes",) + key, [P, W], U32)
-            scales = sb(("scales",) + key, [P, W], U8)
+            codes = sb(("codes",) + key, [P, W], U32, align=256)
+            scales = sb(("scales",) + key, [P, W], U8, align=256)
             cols = slice(first, first + count)
             nc.vector.quantize_mx(out=codes[:, cols].bitcast(FP8X4), scales=scales[:, cols], in_=source[:, 4 * first : 4 * (first + count)])
 
@@ -59,8 +59,8 @@ def tile_magic_landmark_imputation_s3_kernel(tc, x, y, a, b_words, b_scales, r, 
             quantize(("ones",), ones, 0, P)
             make_identity(nc, sb(("ident32",), [P, P], F32)[:])
             make_identity(nc, sb(("ident16",), [P, P], BF16)[:])
-            nc.vector.memset(sb(("b_plane",), [P, 4 * L], U8)[:].bitcast(I32), 0)
-            nc.vector.memset(sb(("d_plane",), [P, 2 * M], U8)[:].bitcast(I32), 0)
+            nc.vector.memset(sb(("b_plane",), [P, 4 * L], U8, align=256)[:].bitcast(I32), 0)
+            nc.vector.memset(sb(("d_plane",), [P, 2 * M], U8, align=256)[:].bitcast(I32), 0)
             nc.scalar.dma_start(out=sb(("r_raw",), [P, 8], BF16)[:].rearrange("p (g w) -> p g w", g=2), in_=r.rearrange("(g p w) -> p g w", g=2, w=4))
             nc.scalar.dma_start(out=sb(("mu_raw",), [P, 8], BF16)[:], in_=mu.rearrange("(p w) -> p w", w=8))
             nc.scalar.dma_start(out=t["lib_rows",][0:8, :], in_=lib.rearrange("(j p) -> j p", p=P))
@@ -105,7 +105,7 @@ def tile_magic_landmark_imputation_s3_kernel(tc, x, y, a, b_words, b_scales, r, 
             nc.sync.dma_start(out=sb(("raw", c, h), [P, 4, W], BF16)[:], in_=rows.rearrange("(p t) g -> p t g", t=4))
 
         def load_b(k):
-            nc.sync.dma_start(out=sb(("b", k), [P, 2 * L], U8)[:].bitcast(I32), in_=b_words[k].bitcast(I32))
+            nc.sync.dma_start(out=sb(("b", k), [P, 2 * L], U8, align=256)[:].bitcast(I32), in_=b_words[k].bitcast(I32))
 
         def load_scales(plane, scales, groups):
             rows = scales.bitcast(I32).rearrange("g (q r) n -> r q g n", r=4)
@@ -118,7 +118,7 @@ def tile_magic_landmark_imputation_s3_kernel(tc, x, y, a, b_words, b_scales, r, 
         def load_d():
             load_scales(t["d_plane",], d_scales, 2)
             nc.sync.dma_start(
-                out=sb(("d",), [P, 4 * M], U8)[:].bitcast(I32).rearrange("p (g n) -> p g n", g=2),
+                out=sb(("d",), [P, 4 * M], U8, align=256)[:].bitcast(I32).rearrange("p (g n) -> p g n", g=2),
                 in_=d_words.bitcast(I32).rearrange("g p n -> p g n"),
             )
 
@@ -139,7 +139,7 @@ def tile_magic_landmark_imputation_s3_kernel(tc, x, y, a, b_words, b_scales, r, 
             )
 
         def empty_a(G, c, jp, engine):
-            unturn(engine, sb(("a_woven", G, c), [P, 4 * W], BF16), 2 * jp, 2, t["a_turned", G, c, jp])
+            unturn(engine, sb(("a_woven", G, c), [P, 4 * W], BF16, "stage%d" % (2 * G + c)), 2 * jp, 2, t["a_turned", G, c, jp])
 
         def quant_a(G, c, jps):
             quantize(("a", G, c), t["a_woven", G, c], 256 * jps[0], 256 * len(jps))
@@ -155,20 +155,20 @@ def tile_magic_landmark_imputation_s3_kernel(tc, x, y, a, b_words, b_scales, r, 
             interleave(engine, sb(("woven", c, h), [P, 4 * W], BF16, "woven%d" % c), t["raw", c, h], half)
 
         def weave_h(h, half, engine):
-            interleave(engine, sb(("h_woven", h, 0), [P, 4 * W], BF16, "h_woven0"), t["h_rows", h], half)
+            interleave(engine, sb(("h_woven", h, 0), [P, 4 * W], BF16, "stage1"), t["h_rows", h], half)
 
         def quant_act(c, h, halves):
             quantize(("act", c, h), t["woven", c, h], 256 * halves[0], 256 * len(halves))
 
         def sort_b(k):
             nc.vector.tensor_copy(
-                out=sb(("b_sorted", k), [P, 2 * W], U8)[:].rearrange("p (t m b) -> p t m b", t=4, b=2),
+                out=sb(("b_sorted", k), [P, 2 * W], U8, align=256)[:].rearrange("p (t m b) -> p t m b", t=4, b=2),
                 in_=t["b", k][:, : 2 * W].rearrange("p (m t b) -> p t m b", t=4, b=2),
             )
 
         def sort_scales(k):
             nc.vector.tensor_copy(
-                out=sb(("b_scales_sorted", k), [P, W], U8)[:].rearrange("p (t m) -> p t m", t=4),
+                out=sb(("b_scales_sorted", k), [P, W], U8, align=256)[:].rearrange("p (t m) -> p t m", t=4),
                 in_=t["b_plane",][:, L * k : L * k + W].rearrange("p (m t) -> p t m", t=4),
             )
 
@@ -197,7 +197,7 @@ def tile_magic_landmark_imputation_s3_kernel(tc, x, y, a, b_words, b_scales, r, 
 
         def empty_unit(h, j, G):
             if G == 0:
-                rows = sb(("h_rows", h), [P, 4, W], BF16, "h_rows")
+                rows = sb(("h_rows", h), [P, 4, W], BF16, "stage0")
                 nc.scalar.activation(out=rows[:, j, :], in_=t["unit", h, j, G][:], func=COPY, scale=t["r_column",][:, j : j + 1])
             else:
                 nc.vector.tensor_tensor(
@@ -216,7 +216,7 @@ def tile_magic_landmark_imputation_s3_kernel(tc, x, y, a, b_words, b_scales, r, 
                     nc.tensor.transpose(turned[:, slot * P : (slot + 1) * P], words[:, u * P : (u + 1) * P], t["ident32",][:])
 
         def empty_h(h, G, gts, engine):
-            unturn(engine, sb(("h_woven", h, G), [P, 4 * W], BF16, "h_woven%d" % G), gts[0], len(gts), t["h_turned", h, G, gts])
+            unturn(engine, sb(("h_woven", h, G), [P, 4 * W], BF16, "stage2"), gts[0], len(gts), t["h_turned", h, G, gts])
 
         def quant_h(h, G, gts):
             quantize(("h", h, G), t["h_woven", h, G], P * gts[0], P * len(gts))
@@ -247,9 +247,9 @@ def tile_magic_landmark_imputation_s3_kernel(tc, x, y, a, b_words, b_scales, r, 
 
         prologue(0)
         load_a(0, 0); load_act(0, 0); load_a(0, 1); load_a(1, 0); load_act(1, 0); load_a(1, 1)
-        load_b_scales()
-        for k in range(4):
-            load_b(k); load_act(2 + k, 0)
+        load_act(2, 0); load_b_scales(); load_b(0)
+        for k in range(1, 4):
+            load_act(2 + k, 0); load_b(k)
         for c in range(6):
             load_act(c, 1)
         load_d()
@@ -267,20 +267,17 @@ def tile_magic_landmark_imputation_s3_kernel(tc, x, y, a, b_words, b_scales, r, 
         for j in range(2, 4): mm1(0, j, 0, 0, j)
         weave(1, 0, 0, V); quant_a(0, 1, (1,)); weave(1, 0, 1, V); quant_a(1, 0, (0,)); quant_act(1, 0, (0, 1)); quant_a(1, 1, (0,))
         turn_a(1, 0, 1, 6); turn_a(1, 1, 1, 7); empty_a(1, 0, 1, S); empty_a(1, 1, 1, S)
-        sort_scales(0); quant_a(1, 0, (1,)); sort_b(0); quant_a(1, 1, (1,))
+        quant_a(1, 0, (1,)); weave(2, 0, 0, V); quant_a(1, 1, (1,)); sort_scales(0)
         for j in range(4): mm1(0, j, 0, 1)
         for gt in range(4): mm1(0, gt, 1, 0, 4 + gt)
         for gt in range(4): mm1(0, gt, 1, 1)
         for c in range(2, 6):
-            weave(c, 0, 0, V); weave(c, 0, 1, S)
-            if c < 5: sort_scales(c - 1)
-            quant_act(c, 0, (0,)); quant_act(c, 0, (1,))
-            if c < 4: sort_b(c - 1)
+            weave(c, 0, 1, S); quant_act(c, 0, (0,)); quant_act(c, 0, (1,)); sort_b(c - 2)
+            if c < 5: weave(c + 1, 0, 0, V); sort_scales(c - 1)
             if c < 4:
                 for gt in range(4): mm1(0, gt, 1, c)
                 for j in range(4): mm1(0, j, 0, c)
             if c < 5: scale_mu(0, c - 2)
-        sort_b(3)
         order = [(1, 0), (1, 1), (0, 0), (0, 1), (0, 2), (0, 3), (1, 2), (1, 3)]
         weave(0, 1, 0, V); weave(0, 1, 1, S); weave(1, 1, 1, S)
         for G, gt in order[:4]: mm1(0, gt, G, 4)

from contextlib import ExitStack

import concourse.mybir as mybir
from concourse.masks import make_identity

M, K, L, G_ALL = 1024, 2048, 1024, 1024
FLOPS = 2 * L * G_ALL * (M + K) + 2 * M * G_ALL * L

F32 = mybir.dt.float32
BF16 = mybir.dt.bfloat16
I32 = mybir.dt.int32
U32 = mybir.dt.uint32
U8 = mybir.dt.uint8
FP8X4 = mybir.dt.float8_e4m3fn_x4
FP4X4 = mybir.dt.float4_e2m1fn_x4
MULT = mybir.AluOpType.mult
ADD = mybir.AluOpType.add
COPY = mybir.ActivationFunctionType.Copy

P = 128
W = 512
V, S = "vector", "scalar"


def tile_magic_landmark_imputation_s3_kernel(tc, x, y, a, b_words, b_scales, r, d_words, d_scales, mu, lib, out):
    nc = tc.nc
    with ExitStack() as ctx:
        keep = ctx.enter_context(tc.tile_pool(name="keep", bufs=1))
        psum = ctx.enter_context(tc.psum_pool(name="psum", bufs=1))
        ctx.enter_context(tc.manual_schedule())
        t = {}

        def sb(key, shape, dtype, tag=None, align=64):
            if key not in t:
                name = "%s%d" % (key[0], len(t))
                t[key] = keep.tile(shape, dtype, name=name, tag=tag or name, align_bytes=align)
            return t[key]

        def bank_tile(key, bank, dtype=F32, width=W):
            t[key] = psum.tile([P, width], dtype, name="%s%d" % (key[0], len(t)), tag="bank%d" % bank)
            return t[key]

        def copy(engine, out, in_):
            if engine == V:
                nc.vector.tensor_copy(out=out, in_=in_)
            else:
                nc.scalar.copy(out=out, in_=in_)

        def quantize(key, source, first, count):
            codes = sb(("codes",) + key, [P, W], U32, align=256)
            scales = sb(("scales",) + key, [P, W], U8, align=256)
            cols = slice(first, first + count)
            nc.vector.quantize_mx(out=codes[:, cols].bitcast(FP8X4), scales=scales[:, cols], in_=source[:, 4 * first : 4 * (first + count)])

        def prologue(n):
            nc.gpsimd.memset(sb(("lib_rows",), [P, P], BF16)[:], 0.0)
            ones = sb(("ones",), [P, W], BF16)
            nc.gpsimd.memset(ones[:], 1.0)
            quantize(("ones",), ones, 0, P)
            make_identity(nc, sb(("ident32",), [P, P], F32)[:])
            make_identity(nc, sb(("ident16",), [P, P], BF16)[:])
            nc.vector.memset(sb(("b_plane",), [P, 4 * L], U8, align=256)[:].bitcast(I32), 0)
            nc.vector.memset(sb(("d_plane",), [P, 2 * M], U8, align=256)[:].bitcast(I32), 0)
            nc.scalar.dma_start(out=sb(("r_raw",), [P, 8], BF16)[:].rearrange("p (g w) -> p g w", g=2), in_=r.rearrange("(g p w) -> p g w", g=2, w=4))
            nc.scalar.dma_start(out=sb(("mu_raw",), [P, 8], BF16)[:], in_=mu.rearrange("(p w) -> p w", w=8))
            nc.scalar.dma_start(out=t["lib_rows",][0:8, :], in_=lib.rearrange("(j p) -> j p", p=P))
            nc.vector.tensor_copy(out=sb(("r_column",), [P, 4], F32)[:], in_=t["r_raw",][:, 0:4])
            nc.scalar.activation(out=sb(("unused",), [P, 1], F32)[:], in_=ones[:, 0:1], func=COPY, scale=2.0)

        def warm_up(n, bank_index):
            bank = bank_tile(("warm", len(t)), bank_index)
            codes, scales = t["codes", "ones"][:, :P].bitcast(FP8X4), t["scales", "ones"][:, :P]
            for i in range(n):
                nc.tensor.matmul_mx(out=bank[:, (i % 4) * P : (i % 4 + 1) * P], lhsT=codes, lhsT_scale=scales, rhs=codes, rhs_scale=scales, start=True, stop=True)

        def spread(name, bank):
            if name == "lib":
                nc.tensor.transpose(bank_tile(("spread", name), bank, BF16, P)[:], t["lib_rows",][:], t["ident16",][:])
            else:
                words = t[name + "_raw",][:].bitcast(F32)
                turned = bank_tile(("spread", name), bank)
                for slot, j in enumerate(range(2 if name == "r" else 0, 4)):
                    nc.tensor.transpose(turned[:, slot * P : (slot + 1) * P], words[:, j : j + 1].to_broadcast([P, P]), t["ident32",][:])

        def keep_spread(name, engine):
            turned = t["spread", name]
            if name == "lib":
                copy(engine, sb(("lib",), [P, 8], F32)[:], turned[:, 0:8])
            elif name == "r":
                copy(engine, sb(("r",), [P, W], BF16)[:].bitcast(F32), turned[:, : 2 * P])
            else:
                words = sb(("mu",), [P, G_ALL], BF16)[:].bitcast(F32)
                copy(engine, words.rearrange("p (n j) -> p n j", j=4), turned[:].rearrange("p (j n) -> p n j", j=4))

        def load_a(G, jp):
            if G == 0:
                rows = a[:W, :].rearrange("(p t) k -> p t k", t=4)[:, 2 * jp : 2 * jp + 2, :]
            else:
                rows = a[W + 256 * jp : W + 256 * (jp + 1), :].rearrange("(j p) k -> p j k", p=P)
            nc.sync.dma_start(out=sb(("a_raw", G, jp), [P, 2, M], BF16)[:], in_=rows)

        def load_act(c, h):
            source, first = (x, W * c) if c < 2 else (y, W * (c - 2))
            rows = source[first : first + W, W * h : W * (h + 1)]
            nc.sync.dma_start(out=sb(("raw", c, h), [P, 4, W], BF16)[:], in_=rows.rearrange("(p t) g -> p t g", t=4))

        def load_b(k):
            nc.sync.dma_start(out=sb(("b", k), [P, 2 * L], U8, align=256)[:].bitcast(I32), in_=b_words[k].bitcast(I32))

        def load_scales(plane, scales, groups):
            rows = scales.bitcast(I32).rearrange("g (q r) n -> r q g n", r=4)
            for r in range(4):
                nc.sync.dma_start(out=plane[r:P:32, :].bitcast(I32).rearrange("q (g n) -> q g n", g=groups), in_=rows[r])

        def load_b_scales():
            load_scales(t["b_plane",], b_scales, 4)

        def load_d():
            load_scales(t["d_plane",], d_scales, 2)
            nc.sync.dma_start(
                out=sb(("d",), [P, 4 * M], U8, align=256)[:].bitcast(I32).rearrange("p (g n) -> p g n", g=2),
                in_=d_words.bitcast(I32).rearrange("g p n -> p g n"),
            )

        def turn_a(G, c, jp, bank):
            turned = bank_tile(("a_turned", G, c, jp), bank)
            words = t["a_raw", G, jp][:].rearrange("p j k -> p (j k)").bitcast(F32)
            for j in range(2):
                for u in range(2):
                    slot = 2 * j + u
                    nc.tensor.transpose(turned[:, slot * P : (slot + 1) * P], words[:, W * j + 256 * c + u : W * j + 256 * (c + 1) : 2], t["ident32",][:])

        def unturn(engine, woven, first, count, turned):
            words = woven[:].bitcast(F32)[:, 256 * first : 256 * (first + count)]
            copy(
                engine,
                words.rearrange("p (j n u) -> p j n u", j=count, u=2),
                turned[:, : 256 * count].rearrange("p (j u n) -> p j n u", j=count, u=2),
            )

        def empty_a(G, c, jp, engine):
            unturn(engine, sb(("a_woven", G, c), [P, 4 * W], BF16, "stage%d" % (2 * G + c)), 2 * jp, 2, t["a_turned", G, c, jp])

        def quant_a(G, c, jps):
            quantize(("a", G, c), t["a_woven", G, c], 256 * jps[0], 256 * len(jps))

        def interleave(engine, woven, rows, half):
            copy(
                engine,
                woven[:, 1024 * half : 1024 * (half + 1)].rearrange("p (c i t) -> p c t i", i=4, t=4),
                rows[:, :, 256 * half : 256 * (half + 1)].rearrange("p t (c i) -> p c t i", i=4),
            )

        def weave(c, h, half, engine):
            interleave(engine, sb(("woven", c, h), [P, 4 * W], BF16, "woven%d" % c), t["raw", c, h], half)

        def weave_h(h, half, engine):
            interleave(engine, sb(("h_woven", h, 0), [P, 4 * W], BF16, "stage1"), t["h_rows", h], half)

        def quant_act(c, h, halves):
            quantize(("act", c, h), t["woven", c, h], 256 * halves[0], 256 * len(halves))

        def sort_b(k):
            nc.vector.tensor_copy(
                out=sb(("b_sorted", k), [P, 2 * W], U8, align=256)[:].rearrange("p (t m b) -> p t m b", t=4, b=2),
                in_=t["b", k][:, : 2 * W].rearrange("p (m t b) -> p t m b", t=4, b=2),
            )

        def sort_scales(k):
            nc.vector.tensor_copy(
                out=sb(("b_scales_sorted", k), [P, W], U8, align=256)[:].rearrange("p (t m) -> p t m", t=4),
                in_=t["b_plane",][:, L * k : L * k + W].rearrange("p (m t) -> p t m", t=4),
            )

        def mm1(h, j, G, c, bank=None):
            if bank is not None:
                bank_tile(("unit", h, j, G), bank)
            cols = slice(P * j, P * (j + 1)) if G == 1 else slice(0, W)
            genes = (t["codes", "act", c, h][:, cols].bitcast(FP8X4), t["scales", "act", c, h][:, cols])
            cols = slice(P * j, P * (j + 1)) if G == 0 else slice(0, W)
            if c < 2:
                marks = (t["codes", "a", G, c][:, cols].bitcast(FP8X4), t["scales", "a", G, c][:, cols])
            elif G == 0:
                marks = (t["b_sorted", c - 2][:, 2 * cols.start : 2 * cols.stop].bitcast(FP4X4), t["b_scales_sorted", c - 2][:, cols])
            else:
                marks = (t["b", c - 2][:, 2 * W :].bitcast(FP4X4), t["b_plane",][:, L * (c - 2) + W : L * (c - 1)])
            still, moving = (marks, genes) if G == 0 else (genes, marks)
            nc.tensor.matmul_mx(
                out=t["unit", h, j, G][:],
                lhsT=still[0],
                lhsT_scale=still[1],
                rhs=moving[0],
                rhs_scale=moving[1],
                start=(c == 0),
                stop=(c == 5),
            )

        def empty_unit(h, j, G):
            if G == 0:
                rows = sb(("h_rows", h), [P, 4, W], BF16, "stage0")
                nc.scalar.activation(out=rows[:, j, :], in_=t["unit", h, j, G][:], func=COPY, scale=t["r_column",][:, j : j + 1])
            else:
                nc.vector.tensor_tensor(
                    out=sb(("ht", h, j), [P, W], BF16, "ht%d" % j)[:].rearrange("g (u p e) -> g u p e", u=2, e=2),
                    in0=t["unit", h, j, G][:].rearrange("g (p u e) -> g u p e", u=2, e=2),
                    in1=t["r",][:].rearrange("g (u p e) -> g u p e", u=2, e=2),
                    op=MULT,
                )

        def turn_h(h, G, gts, bank):
            turned = bank_tile(("h_turned", h, G, gts), bank)
            for j, gt in enumerate(gts):
                words = t["ht", h, gt][:].bitcast(F32)
                for u in range(2):
                    slot = 2 * j + u
                    nc.tensor.transpose(turned[:, slot * P : (slot + 1) * P], words[:, u * P : (u + 1) * P], t["ident32",][:])

        def empty_h(h, G, gts, engine):
            unturn(engine, sb(("h_woven", h, G), [P, 4 * W], BF16, "stage2"), gts[0], len(gts), t["h_turned", h, G, gts])

        def quant_h(h, G, gts):
            quantize(("h", h, G), t["h_woven", h, G], P * gts[0], P * len(gts))

        def scale_mu(h, mt):
            nc.scalar.activation(out=sb(("o", h, mt), [P, W], F32)[:], in_=t["mu",][:, W * h : W * (h + 1)], func=COPY, scale=t["lib",][:, mt : mt + 1])

        def mm2(h, mt, G, bank=None):
            if bank is not None:
                bank_tile(("z", h, mt), bank)
            nc.tensor.matmul_mx(
                out=t["z", h, mt][:],
                lhsT=t["d",][:, 2 * (M * G + P * mt) : 2 * (M * G + P * (mt + 1))].bitcast(FP4X4),
                lhsT_scale=t["d_plane",][:, M * G + P * mt : M * G + P * (mt + 1)],
                rhs=t["codes", "h", h, G][:].bitcast(FP8X4),
                rhs_scale=t["scales", "h", h, G][:],
                start=(G == 0),
                stop=(G == 1),
            )

        def finish(h, mt, pieces=1):
            width = W // pieces
            for first in range(0, W, width):
                o = t["o", h, mt][:, first : first + width]
                z = t["z", h, mt][:, first : first + width]
                nc.vector.scalar_tensor_tensor(out=o, in0=z, scalar=t["lib",][:, mt : mt + 1], in1=o, op0=MULT, op1=ADD)
                nc.sync.dma_start(out=out[P * mt : P * (mt + 1), W * h + first : W * h + first + width], in_=o)

        prologue(0)
        load_a(0, 0); load_act(0, 0); load_a(0, 1); load_a(1, 0); load_act(1, 0); load_a(1, 1)
        load_act(2, 0); load_b_scales(); load_b(0)
        for k in range(1, 4):
            load_act(2 + k, 0); load_b(k)
        for c in range(6):
            load_act(c, 1)
        load_d()
        warm_up(15, 3)
        turn_a(0, 0, 0, 4); turn_a(0, 1, 0, 5); empty_a(0, 0, 0, S); empty_a(0, 1, 0, S)
        warm_up(3, 3)
        spread("r", 0); spread("mu", 1); spread("lib", 2)
        warm_up(4, 3)
        weave(0, 0, 0, V); weave(0, 0, 1, V); quant_a(0, 0, (0,)); quant_act(0, 0, (0, 1))
        keep_spread("r", S); keep_spread("lib", V)
        turn_a(0, 0, 1, 6); turn_a(0, 1, 1, 7); keep_spread("mu", S); empty_a(0, 0, 1, S); empty_a(0, 1, 1, S)
        quant_a(0, 1, (0,)); quant_a(0, 0, (1,))
        for j in range(2): mm1(0, j, 0, 0, j)
        turn_a(1, 0, 0, 4); turn_a(1, 1, 0, 5); empty_a(1, 0, 0, S); empty_a(1, 1, 0, S)
        for j in range(2, 4): mm1(0, j, 0, 0, j)
        weave(1, 0, 0, V); quant_a(0, 1, (1,)); weave(1, 0, 1, V); quant_a(1, 0, (0,)); quant_act(1, 0, (0, 1)); quant_a(1, 1, (0,))
        turn_a(1, 0, 1, 6); turn_a(1, 1, 1, 7); empty_a(1, 0, 1, S); empty_a(1, 1, 1, S)
        quant_a(1, 0, (1,)); weave(2, 0, 0, V); quant_a(1, 1, (1,)); sort_scales(0)
        for j in range(4): mm1(0, j, 0, 1)
        for gt in range(4): mm1(0, gt, 1, 0, 4 + gt)
        for gt in range(4): mm1(0, gt, 1, 1)
        for c in range(2, 6):
            weave(c, 0, 1, S); quant_act(c, 0, (0,)); quant_act(c, 0, (1,)); sort_b(c - 2)
            if c < 5: weave(c + 1, 0, 0, V); sort_scales(c - 1)
            if c < 4:
                for gt in range(4): mm1(0, gt, 1, c)
                for j in range(4): mm1(0, j, 0, c)
            if c < 5: scale_mu(0, c - 2)
        order = [(1, 0), (1, 1), (0, 0), (0, 1), (0, 2), (0, 3), (1, 2), (1, 3)]
        weave(0, 1, 0, V); weave(0, 1, 1, S); weave(1, 1, 1, S)
        for G, gt in order[:4]: mm1(0, gt, G, 4)
        for i, (G, gt) in enumerate(order):
            if i >= 4: mm1(0, gt, G, 4)
            mm1(0, gt, G, 5); empty_unit(0, gt, G)
            if i == 0: quant_act(0, 1, (0, 1)); weave(1, 1, 0, V)
            if i == 1: quant_act(1, 1, (0, 1)); weave(2, 1, 0, V)
            if i == 5: weave(2, 1, 1, S); weave(3, 1, 1, S)
            if i == 6: weave(3, 1, 0, V); quant_act(2, 1, (0, 1))
        def row(c, units):
            for G, gt in units: mm1(1, gt, G, c, 4 * G + gt if c == 0 else None)
        six = order[:6]
        row(0, six); row(1, six)
        weave(4, 1, 0, V); quant_act(3, 1, (0, 1)); weave(4, 1, 1, S)
        row(2, six)
        turn_h(0, 1, (0, 1), 6); turn_h(0, 1, (2, 3), 7)
        weave(5, 1, 0, V); weave(5, 1, 1, S); quant_act(4, 1, (0, 1))
        empty_h(0, 1, (0, 1), S); empty_h(0, 1, (2, 3), S)
        weave_h(0, 0, V); quant_act(5, 1, (0, 1)); weave_h(0, 1, V); quant_h(0, 1, (0, 1, 2, 3)); quant_h(0, 0, (0, 1, 2, 3))
        row(3, six)
        for mt in range(3, 8): scale_mu(0, mt)
        zb = (6, 7, 4, 5, 7, 4, 1, 3)
        def z0(mt):
            mm2(0, mt, 0, zb[mt]); mm2(0, mt, 1)
        for G, gt in [(0, 0), (0, 1), (0, 2), (0, 3), (1, 0), (1, 1)]:
            mm1(1, gt, G, 4); mm1(1, gt, G, 5); empty_unit(1, gt, G)
        z0(0); z0(1); finish(0, 0); finish(0, 1)
        weave_h(1, 0, S); weave_h(1, 1, V)
        for mt in range(4): scale_mu(1, mt)
        def unit(gt, bank):
            for c in range(6): mm1(1, gt, 1, c, bank if c == 0 else None)
        unit(2, 2); empty_unit(1, 2, 1)
        z0(2); z0(3); finish(0, 2); quant_h(1, 0, (0, 1, 2, 3))
        turn_h(1, 1, (0, 1), 3); turn_h(1, 1, (2,), 1)
        empty_h(1, 1, (0, 1), S); empty_h(1, 1, (2,), S)
        for mt in range(4, 6): scale_mu(1, mt)
        finish(0, 3)
        unit(3, 6); quant_h(1, 1, (0, 1)); quant_h(1, 1, (2,)); empty_unit(1, 3, 1)
        z0(4); z0(5)
        turn_h(1, 1, (3,), 0); empty_h(1, 1, (3,), S)
        for mt in range(6, 8): scale_mu(1, mt)
        finish(0, 4); finish(0, 5)
        z0(6); z0(7)
        quant_h(1, 1, (3,))
        finish(0, 6); finish(0, 7)
        banks = (5, 2, 6, 7, 4, 0, 1, 3)
        for mt in range(8):
            mm2(1, mt, 0, banks[mt]); mm2(1, mt, 1); finish(1, mt)
